import numpy as np
import ml_dtypes


def mxq(x, axis, fmt="e4m3"):
    dtype, down = {"e4m3": (ml_dtypes.float8_e4m3fn, 7), "e5m2": (ml_dtypes.float8_e5m2, 14)}[fmt]
    v = np.moveaxis(np.asarray(x, np.float32).astype(ml_dtypes.bfloat16).astype(np.float64), axis, -1)
    blocks = v.reshape(v.shape[:-1] + (-1, 32))
    amax = np.abs(blocks).max(-1, keepdims=True)
    byte = np.maximum(np.where(amax > 0, np.frexp(amax)[1] - 1 + 127, 0) - down, 1)
    scale = np.exp2(byte - 127.0)
    codes = (blocks / scale).astype(np.float32).astype(dtype).astype(np.float64)
    return np.moveaxis((codes * scale).reshape(v.shape), -1, axis)


WIDE = False


def mx_kscale(k):
    if not WIDE:
        return np.ones(k)
    levels = np.array([10, -10, 5, -5, 0])
    if k % 512:
        return np.exp2(np.random.permutation(np.resize(levels, k // 32))).repeat(32)
    a = np.empty((k // 512, 16))
    for p in range(k // 512):
        a[p, :8] = np.random.permutation(np.resize(levels, 8))
        for g in range(8):
            far = levels[np.abs(levels - a[p, g]) >= 10]
            a[p, g + 8] = far[np.random.randint(len(far))]
    return np.exp2(a.ravel()).repeat(32)


def f64(x):
    return np.asarray(x).astype(np.float64)


def striped(idx):
    return np.tile(idx.reshape(-1, 16).T, (8, 1)).astype(np.uint16)


def unstriped(offs):
    return offs[:16].T.reshape(-1).astype(np.int64)


def pack_weight(w):
    k, n = w.shape
    w = f64(np.asarray(w, np.float32).astype(ml_dtypes.bfloat16)).reshape(k // 32, 32, n)
    amax = np.abs(w).max(1)
    byte = np.clip(np.where(amax > 0, np.frexp(amax)[1] - 1 + 127 - 7, 1), 1, 254)
    scaled = (w * np.exp2(127.0 - byte)[:, None, :]).reshape(k, n).astype(np.float32)
    words = np.ascontiguousarray(scaled.reshape(k // 512, 128, 4, n).transpose(0, 1, 3, 2)).astype(ml_dtypes.float8_e4m3fn).view(np.uint8)
    return words, np.ascontiguousarray(byte.astype(np.uint8).reshape(k // 512, 16, n))


def unpack_weight(words, scales):
    g, p, n, _ = words.shape
    vals = np.ascontiguousarray(words).view(ml_dtypes.float8_e4m3fn).astype(np.float64) * np.repeat(np.exp2(scales.astype(np.float64) - 127.0), 8, axis=1)[..., None]
    return vals.transpose(0, 1, 3, 2).reshape(g * 512, n)


E2M1 = np.array([0.0, 0.5, 1.0, 1.5, 2.0, 3.0, 4.0, 6.0, -0.0, -0.5, -1.0, -1.5, -2.0, -3.0, -4.0, -6.0])


def pack_fp4(w):
    k, n = w.shape
    w = f64(np.asarray(w, np.float32).astype(ml_dtypes.bfloat16)).reshape(k // 32, 32, n)
    amax = np.abs(w).max(1)
    mant, ex = np.frexp(amax / 6.0)
    byte = np.clip(np.where(amax > 0, np.where(mant > 0.5, ex, ex - 1) + 127, 1), 1, 254)
    scaled = (w * np.exp2(127.0 - byte)[:, None, :]).reshape(k, n).astype(np.float32)
    c = np.ascontiguousarray(scaled.reshape(k // 512, 128, 4, n).transpose(0, 1, 3, 2)).astype(ml_dtypes.float4_e2m1fn).view(np.uint8) & 0xF
    words = (c[..., 0::2] | (c[..., 1::2] << 4)).reshape(k // 512, 128, 2 * n)
    return np.ascontiguousarray(words), np.ascontiguousarray(byte.astype(np.uint8).reshape(k // 512, 16, n))


def unpack_fp4(words, scales):
    g, _, n = scales.shape
    words = np.ascontiguousarray(words).reshape(g, 128, n, 2)
    nib = np.empty((g, 128, n, 4), np.uint8)
    nib[..., 0::2] = words & 0xF
    nib[..., 1::2] = words >> 4
    vals = E2M1[nib] * np.repeat(np.exp2(scales.astype(np.float64) - 127.0), 8, axis=1)[..., None]
    return vals.transpose(0, 1, 3, 2).reshape(g * 512, n)


def relu(v):
    return np.maximum(v, 0.0)


def sigmoid(v):
    return 1.0 / (1.0 + np.exp(-np.maximum(v, -700.0)))


K, T, S, D, H, Z, W = 512, 2048, 512, 2, 512, 512, 2048
P = 2 ** 7


def setup_inputs():
    n = np.random.standard_normal
    s = mx_kscale(K)[:, None]
    u = mx_kscale(H)
    packed_xT = pack_weight(n((K, T)) * s)
    packed_w1 = pack_fp4(n((K, H)) / np.sqrt(K) / s)
    packed_eT = pack_weight(n((K, W)) * s)
    packed_w2 = pack_fp4(n((K, H)) / np.sqrt(K) / s)
    packed_w3 = pack_fp4(n((K, H)) / np.sqrt(K) / s)
    return {
        "x_words": packed_xT[0],
        "x_scales": packed_xT[1],
        "w1_words": packed_w1[0],
        "w1_scales": packed_w1[1],
        "e_words": packed_eT[0],
        "e_scales": packed_eT[1],
        "w2_words": packed_w2[0],
        "w2_scales": packed_w2[1],
        "w3_words": packed_w3[0],
        "w3_scales": packed_w3[1],
        "unit": (np.random.uniform(0.6, 1.4, (H, 1)) * u[:, None]).astype(np.float32),
        "unit2": (np.random.uniform(0.6, 1.4, (H, 1)) / np.sqrt(H) / u[:, None]).astype(np.float32),
        "imm": (np.tile(np.random.uniform(0.3, 1.2, W), (P, 1))).astype(np.float32),
        "offs": striped(np.random.permutation(T)[:S]),
        "agn": striped(np.random.permutation(W)[:Z]),
        "mut": striped(np.random.permutation(Z)),
        "esc": striped(np.random.permutation(Z)),
    }


def reference(x_words, x_scales, w1_words, w1_scales, e_words, e_scales, w2_words, w2_scales, w3_words, w3_scales, unit, unit2, imm, offs, agn, mut, esc):
    xq = unpack_weight(x_words, x_scales)[:, unstriped(offs)]
    y = unpack_fp4(w1_words, w1_scales).T @ xq
    absy = np.abs(y)
    par_ = (y.reshape(len(y), -1, D).sum(axis=2)) / (absy.reshape(len(absy), -1, D).max(axis=2) + 0.5)
    hid = f64(unit) * par_
    e_agn = unpack_weight(e_words, e_scales)[:, unstriped(agn)]
    ye = unpack_fp4(w2_words, w2_scales).T @ e_agn
    yw = unpack_fp4(w3_words, w3_scales).T @ e_agn
    wm = yw[:, unstriped(mut)]
    epi = ye - (0.8 * relu(wm))
    hid2 = f64(unit2) * epi
    sc = mxq(hid, 0, "e4m3").T @ mxq(hid2, 0, "e4m3")
    bind = sigmoid(2.0 * sc)
    be = bind[:, unstriped(esc)]
    db = bind - be
    return db * (f64(imm)[:1][:, unstriped(agn)]) + 0.2 * sc

@@ -1,0 +1,246 @@
+from contextlib import ExitStack
+
+import concourse.mybir as mybir
+from concourse.masks import make_identity
+
+F32 = mybir.dt.float32
+BF16 = mybir.dt.bfloat16
+I32 = mybir.dt.int32
+U32 = mybir.dt.uint32
+U16 = mybir.dt.uint16
+U8 = mybir.dt.uint8
+FP8X4 = mybir.dt.float8_e4m3fn_x4
+FP4X4 = mybir.dt.float4_e2m1fn_x4
+ALU = mybir.AluOpType
+ACT = mybir.ActivationFunctionType
+
+P = 128
+TABLE = 2048
+N = 512
+PACK = 4
+SPARE = 16
+FLOPS = 939524096
+
+
+def tile_picked_yglycan_dif_p_kernel(
+    tc, x_words, x_scales, w1_words, w1_scales, e_words, e_scales, w2_words, w2_scales,
+    w3_words, w3_scales, unit, unit2, imm, offs, agn, mut, esc, out,
+):
+    nc = tc.nc
+    with ExitStack() as ctx:
+        sb = ctx.enter_context(tc.tile_pool(name="sb", bufs=1))
+        ps = ctx.enter_context(tc.psum_pool(name="ps", bufs=1))
+
+        def tile(name, shape, dtype):
+            return sb.tile(shape, dtype, name=name, align_bytes=64)
+
+        def bank(index, shape):
+            return ps.tile(shape, F32, name="bank%d" % index, tag="bank%d" % index)
+
+        lists = {name: tile(name + "_list", [P, N // 16], U16) for name in ("agn", "offs", "mut", "esc")}
+        e_tab, x_tab = tile("e_tab", [P, TABLE], I32), tile("x_tab", [P, TABLE], I32)
+        es_tab, xs_tab = tile("es_tab", [P, TABLE], U8), tile("xs_tab", [P, TABLE], U8)
+        w_raw = {w: tile("w%d_raw" % w, [P, 256], I32) for w in (1, 2, 3)}
+        ws_raw = {w: tile("w%ds_raw" % w, [P, 128], I32) for w in (1, 2, 3)}
+        imm_tab = tile("imm_tab", [P, TABLE], F32)
+        unit_rows = tile("unit_rows", [P, P], F32)
+        ident = tile("ident", [P, P], F32)
+        rect = [tile("rect%d" % t, [P, N + SPARE], F32) for t in range(PACK)]
+
+        nc.vector.memset(es_tab[:].bitcast(I32), 0)
+        nc.vector.memset(ws_raw[3][:], 0)
+        nc.vector.memset(xs_tab[:].bitcast(I32), 0)
+        nc.vector.memset(ws_raw[1][:], 0)
+        nc.vector.memset(ws_raw[2][:], 0)
+        nc.gpsimd.memset(unit_rows[:], 0.0)
+
+        def scale_rows(queue, plane, scales, q):
+            queue.dma_start(out=plane[32 * q : 32 * q + 4, :], in_=scales[0, 4 * q : 4 * q + 4, :].bitcast(I32))
+
+        def table_words(words):
+            return words[0].rearrange("p n t -> p (n t)").bitcast(I32)
+
+        es_i32, xs_i32 = es_tab[:].bitcast(I32), xs_tab[:].bitcast(I32)
+        for row, vec in ((PACK, unit2), (0, unit)):
+            nc.gpsimd.dma_start(
+                out=unit_rows[row : row + PACK, :].rearrange("t (b r) -> t b r", r=8),
+                in_=vec.rearrange("(b t r) o -> t b (r o)", t=PACK, r=8),
+            )
+        make_identity(nc, ident[:])
+        for t in range(PACK):
+            nc.gpsimd.memset(rect[t][:, N:], 0.0)
+        for q in range(4):
+            scale_rows(nc.gpsimd, ws_raw[2], w2_scales, q)
+        nc.sync.dma_start(lists["agn"][:], agn)
+        nc.sync.dma_start(out=w_raw[3][:], in_=w3_words[0].bitcast(I32))
+        nc.sync.dma_start(out=e_tab[:], in_=table_words(e_words))
+        for q in range(4):
+            scale_rows(nc.sync, es_i32, e_scales, q)
+        for q in range(4):
+            scale_rows(nc.sync, ws_raw[3], w3_scales, q)
+        nc.sync.dma_start(lists["offs"][:], offs)
+        for q in range(4):
+            scale_rows(nc.sync, xs_i32, x_scales, q)
+        nc.sync.dma_start(lists["mut"][:], mut)
+        nc.sync.dma_start(out=x_tab[:], in_=table_words(x_words))
+        nc.sync.dma_start(out=w_raw[1][:], in_=w1_words[0].bitcast(I32))
+        for q in range(4):
+            scale_rows(nc.sync, ws_raw[1], w1_scales, q)
+        nc.sync.dma_start(out=w_raw[2][:], in_=w2_words[0].bitcast(I32))
+        nc.sync.dma_start(lists["esc"][:], esc)
+        nc.sync.dma_start(out=imm_tab[:], in_=imm)
+
+        def deal(w):
+            words, scales = tile("w%d" % w, [P, 2 * N], U8), tile("w%ds" % w, [P, N], U8)
+            nc.vector.tensor_copy(
+                out=words[:].bitcast(I32).rearrange("p (t b c) -> p t b c", t=PACK, c=4),
+                in_=w_raw[w][:].rearrange("p (b t c) -> p t b c", t=PACK, c=4),
+            )
+            nc.vector.tensor_copy(
+                out=scales[:].bitcast(I32).rearrange("p (t b c) -> p t b c", t=PACK, c=2),
+                in_=ws_raw[w][:].rearrange("p (b t c) -> p t b c", t=PACK, c=2),
+            )
+            return words, scales
+
+        def pick(name, table, scale_table, offsets):
+            words, scales = tile(name, [P, N], U32), tile(name + "s", [P, N], U8)
+            nc.vector.tensor_copy(scales[:], scale_table[:].indirect(offsets[:]))
+            nc.vector.tensor_copy(words[:], table[:].bitcast(U32).indirect(offsets[:]))
+            return words, scales
+
+        def project(dst, weight, t, picked, cols):
+            nc.tensor.matmul_mx(
+                out=dst,
+                lhsT=weight[0][:, 2 * P * t : 2 * P * (t + 1)].bitcast(FP4X4),
+                lhsT_scale=weight[1][:, P * t : P * (t + 1)],
+                rhs=picked[0][:, cols].bitcast(FP8X4),
+                rhs_scale=picked[1][:, cols],
+                start=True,
+                stop=True,
+            )
+
+        turned = bank(7, [P, P])
+        nc.tensor.transpose(turned[:], unit_rows[:], ident[:])
+        units = tile("units", [P, 2 * PACK], F32)
+        nc.vector.tensor_copy(out=units[:], in_=turned[:, : 2 * PACK])
+        twice = tile("twice", [P, PACK], F32)
+        sgn = tile("sgn", [P, PACK], F32)
+        mag2 = tile("mag2", [P, PACK], F32)
+        mag2_cut = tile("mag2_cut", [P, PACK], F32)
+        unit_sgn = tile("unit_sgn", [P, PACK], F32)
+        nc.vector.tensor_scalar(twice[:], units[:, PACK:], 0.0, 2.0, ALU.is_ge, ALU.mult)
+        nc.vector.scalar_tensor_tensor(mag2[:], units[:, PACK:], -1.0, units[:, PACK:], ALU.mult, ALU.max)
+        nc.vector.tensor_scalar(sgn[:], twice[:], -1.0, None, ALU.add)
+        nc.vector.tensor_scalar(mag2_cut[:], mag2[:], 0.8, None, ALU.mult)
+        nc.vector.tensor_tensor(unit_sgn[:], units[:, :PACK], sgn[:], ALU.mult)
+
+        w3 = deal(3)
+        e_pick = pick("e_pick", e_tab, es_tab, lists["agn"])
+        every = slice(0, N)
+        yw = [bank(t, [P, N]) for t in range(PACK)]
+        for t in range(PACK):
+            project(yw[t][:], w3, t, e_pick, every)
+        w1 = deal(1)
+        x_pick = pick("x_pick", x_tab, xs_tab, lists["offs"])
+        w2 = deal(2)
+        y = [[bank(4 + 2 * h + j, [P, 2, N // 2]) for j in range(2)] for h in range(2)]
+        for h in range(2):
+            for t in range(PACK):
+                project(y[h][t // 2][:, t % 2, :], w1, t, x_pick, slice(256 * h, 256 * (h + 1)))
+
+        mutated = [tile("mutated%d" % t, [P, N], F32) for t in range(PACK)]
+        hid2_rows = tile("hid2_rows", [P, PACK, N], BF16)
+        first = [tile("first%d" % h, [P, PACK, P], F32) for h in range(2)]
+        total = [tile("total%d" % h, [P, PACK, P], F32) for h in range(2)]
+        larger = [tile("larger%d" % h, [P, PACK, P], F32) for h in range(2)]
+        negmax = [tile("negmax%d" % h, [P, PACK, P], F32) for h in range(2)]
+        root = [tile("root%d" % h, [P, PACK, P], F32) for h in range(2)]
+        recip = [tile("recip%d" % h, [P, PACK, P], F32) for h in range(2)]
+        ye = {}
+
+        def rectify(t):
+            nc.scalar.activation(rect[t][:, :N], yw[t][:], ACT.Relu, scale=mag2_cut[:, t : t + 1])
+            ye[t] = bank(t, [P, N])
+            project(ye[t][:], w2, t, e_pick, every)
+
+        def mutate(t):
+            nc.scalar.activation(mutated[t][:], rect[t][:].indirect(lists["mut"][:]), ACT.Copy)
+
+        def epitope(t):
+            nc.vector.scalar_tensor_tensor(hid2_rows[:, t, :], ye[t][:], mag2[:, t : t + 1], mutated[t][:], ALU.mult, ALU.subtract)
+
+        def pairs(h):
+            for j in range(2):
+                both = y[h][j][:].rearrange("p t (v d) -> p t v d", d=2)
+                rows = slice(2 * j, 2 * j + 2)
+                nc.scalar.copy(first[h][:, rows, :], both[:, :, :, 0])
+            for j in range(2):
+                both = y[h][j][:].rearrange("p t (v d) -> p t v d", d=2)
+                rows = slice(2 * j, 2 * j + 2)
+                nc.vector.tensor_tensor(total[h][:, rows, :], both[:, :, :, 1], first[h][:, rows, :], ALU.add)
+                nc.vector.tensor_tensor(larger[h][:, rows, :], both[:, :, :, 1], first[h][:, rows, :], ALU.max)
+            nc.vector.scalar_tensor_tensor(negmax[h][:], total[h][:], 0.0, larger[h][:], ALU.min, ALU.subtract)
+
+        def invert(h):
+            nc.scalar.activation(root[h][:], negmax[h][:], ACT.Abs_reciprocal_sqrt, bias=0.5, scale=-1.0)
+            nc.scalar.activation(recip[h][:], root[h][:], ACT.Square)
+
+        def quantise(name, rows, width):
+            woven = tile(name + "_woven", [P, width, PACK], BF16)
+            nc.vector.tensor_copy(
+                out=woven[:].rearrange("p (c i) t -> p c t i", i=4),
+                in_=rows[:].rearrange("p t (c i) -> p c t i", i=4),
+            )
+            codes, scales = tile(name + "_codes", [P, width], U32), tile(name + "_scales", [P, width], U8)
+            nc.vector.quantize_mx(out=codes[:].bitcast(FP8X4), scales=scales[:], in_=woven[:].rearrange("p w t -> p (w t)"))
+            return codes, scales
+
+        def paratope(h):
+            rows = tile("hid_rows%d" % h, [P, PACK, P], BF16)
+            for t in range(PACK):
+                nc.vector.scalar_tensor_tensor(rows[:, t, :], total[h][:, t, :], unit_sgn[:, t : t + 1], recip[h][:, t, :], ALU.mult, ALU.mult)
+            return quantise("hid%d" % h, rows, P)
+
+        rectify(0)
+        mutate(0)
+        rectify(1)
+        pairs(0)
+        mutate(1)
+        epitope(0)
+        rectify(2)
+        pairs(1)
+        mutate(2)
+        epitope(1)
+        rectify(3)
+        mutate(3)
+        epitope(2)
+        invert(0)
+        invert(1)
+        epitope(3)
+        hid2 = quantise("hid2", hid2_rows, N)
+        imm_pick = tile("imm_pick", [P, N], F32)
+        nc.scalar.activation(imm_pick[:], imm_tab[:].indirect(lists["agn"][:]), ACT.Copy)
+
+        sc = {}
+        for h in range(2):
+            hid = paratope(h)
+            sc[h] = bank(4 + h, [P, N])
+            nc.tensor.matmul_mx(
+                out=sc[h][:], lhsT=hid[0][:].bitcast(FP8X4), lhsT_scale=hid[1][:],
+                rhs=hid2[0][:].bitcast(FP8X4), rhs_scale=hid2[1][:], start=True, stop=True,
+            )
+        for h in range(2):
+            bind = tile("bind%d" % h, [P, N], F32)
+            nc.scalar.activation(bind[:], sc[h][:], ACT.Sigmoid, scale=2.0)
+            for c in range(2):
+                cols = slice(256 * c, 256 * (c + 1))
+                name = "%d_%d" % (h, c)
+                escaped = tile("escaped" + name, [P, 256], F32)
+                drop = tile("drop" + name, [P, 256], F32)
+                weighed = tile("weighed" + name, [P, 256], F32)
+                result = tile("result" + name, [P, 256], F32)
+                nc.scalar.activation(escaped[:], bind[:].indirect(lists["esc"][:, 16 * c : 16 * (c + 1)]), ACT.Copy)
+                nc.vector.tensor_tensor(drop[:], bind[:, cols], escaped[:], ALU.subtract)
+                nc.vector.tensor_tensor(weighed[:], drop[:], imm_pick[:, cols], ALU.mult)
+                nc.vector.scalar_tensor_tensor(result[:], sc[h][:, cols], 0.2, weighed[:], ALU.mult, ALU.add)
+                nc.sync.dma_start(out=out[P * h : P * (h + 1), cols], in_=result[:])

@@ -31,8 +31,8 @@ def tile_picked_yglycan_dif_p_kernel(
         sb = ctx.enter_context(tc.tile_pool(name="sb", bufs=1))
         ps = ctx.enter_context(tc.psum_pool(name="ps", bufs=1))
 
-        def tile(name, shape, dtype):
-            return sb.tile(shape, dtype, name=name, align_bytes=64)
+        def tile(name, shape, dtype, slot=None):
+            return sb.tile(shape, dtype, name=name, tag=slot or name, align_bytes=64)
 
         def bank(index, shape):
             return ps.tile(shape, F32, name="bank%d" % index, tag="bank%d" % index)
@@ -42,71 +42,84 @@ def tile_picked_yglycan_dif_p_kernel(
         es_tab, xs_tab = tile("es_tab", [P, TABLE], U8), tile("xs_tab", [P, TABLE], U8)
         w_raw = {w: tile("w%d_raw" % w, [P, 256], I32) for w in (1, 2, 3)}
         ws_raw = {w: tile("w%ds_raw" % w, [P, 128], I32) for w in (1, 2, 3)}
-        imm_tab = tile("imm_tab", [P, TABLE], F32)
-        unit_rows = tile("unit_rows", [P, P], F32)
+
         ident = tile("ident", [P, P], F32)
         rect = [tile("rect%d" % t, [P, N + SPARE], F32) for t in range(PACK)]
 
-        nc.vector.memset(es_tab[:].bitcast(I32), 0)
-        nc.vector.memset(ws_raw[3][:], 0)
-        nc.vector.memset(xs_tab[:].bitcast(I32), 0)
-        nc.vector.memset(ws_raw[1][:], 0)
-        nc.vector.memset(ws_raw[2][:], 0)
-        nc.gpsimd.memset(unit_rows[:], 0.0)
+        warm = tile("warm", [P, 1], F32)
+        nc.gpsimd.memset(warm[:], 1.0)
+        warmed = tile("warmed", [P, 1], F32)
+        nc.scalar.activation(warmed[:], warm[:], ACT.Abs_reciprocal_sqrt)
 
         def scale_rows(queue, plane, scales, q):
-            queue.dma_start(out=plane[32 * q : 32 * q + 4, :], in_=scales[0, 4 * q : 4 * q + 4, :].bitcast(I32))
+            rows = scales[0, 4 * q : 4 * q + 4, :].bitcast(I32)
+            queue.dma_start(out=plane[32 * q : 32 * (q + 1), :], in_=rows.unsqueeze(0).to_broadcast([8, 4, rows.shape[1]]))
 
         def table_words(words):
             return words[0].rearrange("p n t -> p (n t)").bitcast(I32)
 
         es_i32, xs_i32 = es_tab[:].bitcast(I32), xs_tab[:].bitcast(I32)
-        for row, vec in ((PACK, unit2), (0, unit)):
-            nc.gpsimd.dma_start(
-                out=unit_rows[row : row + PACK, :].rearrange("t (b r) -> t b r", r=8),
-                in_=vec.rearrange("(b t r) o -> t b (r o)", t=PACK, r=8),
-            )
+        def unit_load(queue, name, vec):
+            block = tile(name, [P, 32], F32)
+            queue.dma_start(out=block[:], in_=vec.rearrange("(b c) o -> b (c o)", c=32).unsqueeze(1).to_broadcast([16, 8, 32]))
+            return block
+
+        for q in range(2, 4):
+            scale_rows(nc.gpsimd, ws_raw[1], w1_scales, q)
+        unit_block = unit_load(nc.gpsimd, "unit_block", unit)
         make_identity(nc, ident[:])
         for t in range(PACK):
             nc.gpsimd.memset(rect[t][:, N:], 0.0)
-        for q in range(4):
-            scale_rows(nc.gpsimd, ws_raw[2], w2_scales, q)
-        nc.sync.dma_start(lists["agn"][:], agn)
-        nc.sync.dma_start(out=w_raw[3][:], in_=w3_words[0].bitcast(I32))
-        nc.sync.dma_start(out=e_tab[:], in_=table_words(e_words))
-        for q in range(4):
-            scale_rows(nc.sync, es_i32, e_scales, q)
-        for q in range(4):
-            scale_rows(nc.sync, ws_raw[3], w3_scales, q)
         nc.sync.dma_start(lists["offs"][:], offs)
         for q in range(4):
             scale_rows(nc.sync, xs_i32, x_scales, q)
-        nc.sync.dma_start(lists["mut"][:], mut)
-        nc.sync.dma_start(out=x_tab[:], in_=table_words(x_words))
         nc.sync.dma_start(out=w_raw[1][:], in_=w1_words[0].bitcast(I32))
-        for q in range(4):
+        nc.sync.dma_start(lists["agn"][:], agn)
+        nc.sync.dma_start(out=x_tab[:], in_=table_words(x_words))
+        for q in range(2):
             scale_rows(nc.sync, ws_raw[1], w1_scales, q)
-        nc.sync.dma_start(out=w_raw[2][:], in_=w2_words[0].bitcast(I32))
-        nc.sync.dma_start(lists["esc"][:], esc)
+        for q in range(4):
+            scale_rows(nc.sync, es_i32, e_scales, q)
+        nc.sync.dma_start(out=e_tab[:], in_=table_words(e_words))
+        nc.sync.dma_start(out=w_raw[3][:], in_=w3_words[0].bitcast(I32))
+        for q in range(4):
+            scale_rows(nc.sync, ws_raw[3], w3_scales, q)
+        unit2_block = unit_load(nc.sync, "unit2_block", unit2)
+        nc.sync.dma_start(lists["mut"][:], mut)
+        imm_tab = tile("imm_tab", [P, TABLE], F32)
         nc.sync.dma_start(out=imm_tab[:], in_=imm)
+        nc.sync.dma_start(out=w_raw[2][:], in_=w2_words[0].bitcast(I32))
+        for q in range(4):
+            scale_rows(nc.sync, ws_raw[2], w2_scales, q)
+        nc.sync.dma_start(lists["esc"][:], esc)
 
-        def deal(w):
-            words, scales = tile("w%d" % w, [P, 2 * N], U8), tile("w%ds" % w, [P, N], U8)
-            nc.vector.tensor_copy(
-                out=words[:].bitcast(I32).rearrange("p (t b c) -> p t b c", t=PACK, c=4),
-                in_=w_raw[w][:].rearrange("p (b t c) -> p t b c", t=PACK, c=4),
-            )
-            nc.vector.tensor_copy(
-                out=scales[:].bitcast(I32).rearrange("p (t b c) -> p t b c", t=PACK, c=2),
-                in_=ws_raw[w][:].rearrange("p (b t c) -> p t b c", t=PACK, c=2),
-            )
-            return words, scales
+        own = tile("own", [P, 8], F32)
 
-        def pick(name, table, scale_table, offsets):
-            words, scales = tile(name, [P, N], U32), tile(name + "s", [P, N], U8)
-            nc.vector.tensor_copy(scales[:], scale_table[:].indirect(offsets[:]))
-            nc.vector.tensor_copy(words[:], table[:].bitcast(U32).indirect(offsets[:]))
-            return words, scales
+        def own_factors(name, block, slot=None):
+            masked, factors = tile(name + "_masked", [P, PACK, 8], F32, slot), tile(name, [P, PACK], F32)
+            nc.vector.tensor_tensor(
+                masked[:], block[:].rearrange("p (t r) -> p t r", r=8), own[:].unsqueeze(1).to_broadcast([P, PACK, 8]), ALU.mult
+            )
+            nc.vector.tensor_reduce(factors[:], masked[:], mybir.AxisListType.X, ALU.add)
+            return factors
+
+        def deal(dealt, raw, run):
+            nc.vector.tensor_copy(
+                out=dealt.bitcast(I32).rearrange("p (t b c) -> p t b c", t=PACK, c=run),
+                in_=raw[:].rearrange("p (b t c) -> p t b c", t=PACK, c=run),
+            )
+            return dealt
+
+        def deal_words(w, dealt):
+            return deal(dealt[:, : 2 * N], w_raw[w], 4)
+
+        def deal_scales(w, dealt):
+            return deal(dealt[:, 2 * N :], ws_raw[w], 2)
+
+        def pick(name, window, offsets, dtype):
+            picked = tile(name, [P, N], dtype)
+            nc.vector.tensor_copy(picked[:], window.indirect(offsets[:]))
+            return picked
 
         def project(dst, weight, t, picked, cols):
             nc.tensor.matmul_mx(
@@ -119,116 +132,140 @@ def tile_picked_yglycan_dif_p_kernel(
                 stop=True,
             )
 
-        turned = bank(7, [P, P])
-        nc.tensor.transpose(turned[:], unit_rows[:], ident[:])
-        units = tile("units", [P, 2 * PACK], F32)
-        nc.vector.tensor_copy(out=units[:], in_=turned[:, : 2 * PACK])
-        twice = tile("twice", [P, PACK], F32)
-        sgn = tile("sgn", [P, PACK], F32)
-        mag2 = tile("mag2", [P, PACK], F32)
-        mag2_cut = tile("mag2_cut", [P, PACK], F32)
-        unit_sgn = tile("unit_sgn", [P, PACK], F32)
-        nc.vector.tensor_scalar(twice[:], units[:, PACK:], 0.0, 2.0, ALU.is_ge, ALU.mult)
-        nc.vector.scalar_tensor_tensor(mag2[:], units[:, PACK:], -1.0, units[:, PACK:], ALU.mult, ALU.max)
-        nc.vector.tensor_scalar(sgn[:], twice[:], -1.0, None, ALU.add)
-        nc.vector.tensor_scalar(mag2_cut[:], mag2[:], 0.8, None, ALU.mult)
-        nc.vector.tensor_tensor(unit_sgn[:], units[:, :PACK], sgn[:], ALU.mult)
-
-        w3 = deal(3)
-        e_pick = pick("e_pick", e_tab, es_tab, lists["agn"])
-        every = slice(0, N)
-        yw = [bank(t, [P, N]) for t in range(PACK)]
-        for t in range(PACK):
-            project(yw[t][:], w3, t, e_pick, every)
-        w1 = deal(1)
-        x_pick = pick("x_pick", x_tab, xs_tab, lists["offs"])
-        w2 = deal(2)
+        x_scale_pick = pick("x_scale_pick", xs_tab[:], lists["offs"], U8)
+        w1_tile = tile("w1", [P, 3 * N], U8)
+        w1_dealt = deal_words(1, w1_tile)
+        x_pick = (pick("x_pick", x_tab[:].bitcast(U32), lists["offs"], U32), x_scale_pick)
+        w1 = (w1_dealt, deal_scales(1, w1_tile))
         y = [[bank(4 + 2 * h + j, [P, 2, N // 2]) for j in range(2)] for h in range(2)]
         for h in range(2):
             for t in range(PACK):
                 project(y[h][t // 2][:, t % 2, :], w1, t, x_pick, slice(256 * h, 256 * (h + 1)))
+        e_scale_pick = pick("e_scale_pick", es_tab[:], lists["agn"], U8)
 
-        mutated = [tile("mutated%d" % t, [P, N], F32) for t in range(PACK)]
-        hid2_rows = tile("hid2_rows", [P, PACK, N], BF16)
-        first = [tile("first%d" % h, [P, PACK, P], F32) for h in range(2)]
-        total = [tile("total%d" % h, [P, PACK, P], F32) for h in range(2)]
-        larger = [tile("larger%d" % h, [P, PACK, P], F32) for h in range(2)]
-        negmax = [tile("negmax%d" % h, [P, PACK, P], F32) for h in range(2)]
-        root = [tile("root%d" % h, [P, PACK, P], F32) for h in range(2)]
-        recip = [tile("recip%d" % h, [P, PACK, P], F32) for h in range(2)]
-        ye = {}
+        first, size, total, peak, recip = {}, {}, {}, {}, {}
 
-        def rectify(t):
-            nc.scalar.activation(rect[t][:, :N], yw[t][:], ACT.Relu, scale=mag2_cut[:, t : t + 1])
-            ye[t] = bank(t, [P, N])
-            project(ye[t][:], w2, t, e_pick, every)
+        def members(h, j):
+            return y[h][j][:].rearrange("p t (v d) -> p d t v", d=2)
 
-        def mutate(t):
-            nc.scalar.activation(mutated[t][:], rect[t][:].indirect(lists["mut"][:]), ACT.Copy)
-
-        def epitope(t):
-            nc.vector.scalar_tensor_tensor(hid2_rows[:, t, :], ye[t][:], mag2[:, t : t + 1], mutated[t][:], ALU.mult, ALU.subtract)
-
-        def pairs(h):
+        def take(h):
+            first[h] = tile("first%d" % h, [P, PACK, P], F32)
+            size[h] = tile("size%d" % h, [P, 2, PACK, P], F32)
             for j in range(2):
-                both = y[h][j][:].rearrange("p t (v d) -> p t v d", d=2)
                 rows = slice(2 * j, 2 * j + 2)
-                nc.scalar.copy(first[h][:, rows, :], both[:, :, :, 0])
+                nc.scalar.copy(first[h][:, rows, :], members(h, j)[:, 0])
+                nc.scalar.activation(size[h][:, :, rows, :], members(h, j), ACT.Abs)
+
+        def pairs(h, total_slot, peak_slot):
+            total[h] = tile("total%d" % h, [P, PACK, P], F32, total_slot)
+            peak[h] = tile("peak%d" % h, [P, PACK, P], F32, peak_slot)
+            nc.vector.tensor_tensor(peak[h][:], size[h][:, 0], size[h][:, 1], ALU.max)
             for j in range(2):
-                both = y[h][j][:].rearrange("p t (v d) -> p t v d", d=2)
                 rows = slice(2 * j, 2 * j + 2)
-                nc.vector.tensor_tensor(total[h][:, rows, :], both[:, :, :, 1], first[h][:, rows, :], ALU.add)
-                nc.vector.tensor_tensor(larger[h][:, rows, :], both[:, :, :, 1], first[h][:, rows, :], ALU.max)
-            nc.vector.scalar_tensor_tensor(negmax[h][:], total[h][:], 0.0, larger[h][:], ALU.min, ALU.subtract)
+                nc.vector.tensor_tensor(total[h][:, rows, :], members(h, j)[:, 1], first[h][:, rows, :], ALU.add)
 
-        def invert(h):
-            nc.scalar.activation(root[h][:], negmax[h][:], ACT.Abs_reciprocal_sqrt, bias=0.5, scale=-1.0)
-            nc.scalar.activation(recip[h][:], root[h][:], ACT.Square)
+        def invert(h, slot):
+            root = tile("root%d" % h, [P, PACK, P], F32, slot)
+            recip[h] = tile("recip%d" % h, [P, PACK, P], F32)
+            nc.scalar.activation(root[:], peak[h][:], ACT.Abs_reciprocal_sqrt, bias=0.5)
+            nc.scalar.activation(recip[h][:], root[:], ACT.Square)
 
-        def quantise(name, rows, width):
+        def quantise(name, rows, codes, scales):
+            width = rows.shape[2]
             woven = tile(name + "_woven", [P, width, PACK], BF16)
             nc.vector.tensor_copy(
                 out=woven[:].rearrange("p (c i) t -> p c t i", i=4),
-                in_=rows[:].rearrange("p t (c i) -> p c t i", i=4),
+                in_=rows.rearrange("p t (c i) -> p c t i", i=4),
             )
-            codes, scales = tile(name + "_codes", [P, width], U32), tile(name + "_scales", [P, width], U8)
-            nc.vector.quantize_mx(out=codes[:].bitcast(FP8X4), scales=scales[:], in_=woven[:].rearrange("p w t -> p (w t)"))
-            return codes, scales
+            nc.vector.quantize_mx(out=codes.bitcast(FP8X4), scales=scales, in_=woven[:].rearrange("p w t -> p (w t)"))
 
         def paratope(h):
             rows = tile("hid_rows%d" % h, [P, PACK, P], BF16)
             for t in range(PACK):
                 nc.vector.scalar_tensor_tensor(rows[:, t, :], total[h][:, t, :], unit_sgn[:, t : t + 1], recip[h][:, t, :], ALU.mult, ALU.mult)
-            return quantise("hid%d" % h, rows, P)
+            codes, scales = tile("hid_codes%d" % h, [P, P], U32), tile("hid_scales%d" % h, [P, P], U8)
+            quantise("hid%d" % h, rows[:], codes[:], scales[:])
+            return codes, scales
+
+        take(0)
+        take(1)
+        e_pick = (pick("e_pick", e_tab[:].bitcast(U32), lists["agn"], U32), e_scale_pick)
+        w3_tile = tile("w3", [P, 3 * N], U8)
+        w3 = (deal_words(3, w3_tile), deal_scales(3, w3_tile))
+
+        nc.vector.tensor_reduce(own[:], ident[:].rearrange("p (b r) -> p r b", r=8), mybir.AxisListType.X, ALU.add)
+        u2 = own_factors("u2", unit2_block)
+        twice = tile("twice", [P, PACK], F32)
+        sgn = tile("sgn", [P, PACK], F32)
+        mag2 = tile("mag2", [P, PACK], F32)
+        mag2_cut = tile("mag2_cut", [P, PACK], F32)
+        unit_sgn = tile("unit_sgn", [P, PACK], F32)
+        nc.scalar.activation(mag2_cut[:], u2[:], ACT.Abs, scale=0.8)
+        nc.scalar.activation(mag2[:], u2[:], ACT.Abs)
+        nc.gpsimd.tensor_scalar(twice[:], u2[:], 0.0, 2.0, ALU.is_ge, ALU.mult)
+        nc.gpsimd.tensor_scalar(sgn[:], twice[:], -1.0, None, ALU.add)
+
+        every = slice(0, N)
+        yw = [bank(t, [P, N]) for t in range(PACK)]
+        for t in range(PACK):
+            project(yw[t][:], w3, t, e_pick, every)
+        pairs(0, "w3s_raw", "u2_masked")
+        u1 = own_factors("u1", unit_block, "w3_raw")
+        nc.gpsimd.tensor_tensor(unit_sgn[:], u1[:], sgn[:], ALU.mult)
+        pairs(1, "unit2_block", "size0")
+        imm_pick = tile("imm_pick", [P, N], F32, slot="first0")
+        nc.vector.tensor_copy(imm_pick[:], imm_tab[:].indirect(lists["agn"][:]))
+        w2_tile = tile("w2", [P, 3 * N], U8, slot="first1")
+        w2 = (deal_words(2, w2_tile), deal_scales(2, w2_tile))
+        ye = [bank(4 + t, [P, N]) for t in range(PACK)]
+        for t in range(PACK):
+            project(ye[t][:], w2, t, e_pick, every)
+
+        mutated = [tile("mutated%d" % t, [P, N], F32) for t in range(PACK)]
+        hid2_rows = tile("hid2_rows", [P, PACK, N], BF16)
+
+        def rectify(t):
+            nc.scalar.activation(rect[t][:, :N], yw[t][:], ACT.Relu, scale=mag2_cut[:, t : t + 1])
+
+        def mutate(t, cols):
+            offsets = lists["mut"][:, cols.start // 16 : cols.stop // 16]
+            nc.scalar.activation(mutated[t][:, cols], rect[t][:].indirect(offsets), ACT.Copy)
+
+        def epitope(t, cols):
+            nc.vector.scalar_tensor_tensor(
+                hid2_rows[:, t, cols], ye[t][:, cols], mag2[:, t : t + 1], mutated[t][:, cols], ALU.mult, ALU.subtract
+            )
 
         rectify(0)
-        mutate(0)
-        rectify(1)
-        pairs(0)
-        mutate(1)
-        epitope(0)
-        rectify(2)
-        pairs(1)
-        mutate(2)
-        epitope(1)
-        rectify(3)
-        mutate(3)
-        epitope(2)
-        invert(0)
-        invert(1)
-        epitope(3)
-        hid2 = quantise("hid2", hid2_rows, N)
-        imm_pick = tile("imm_pick", [P, N], F32)
-        nc.scalar.activation(imm_pick[:], imm_tab[:].indirect(lists["agn"][:]), ACT.Copy)
+        mutate(0, every)
+        invert(0, "rect0")
+        hid = {0: paratope(0)}
+        epitope(0, every)
+        for t in range(1, PACK):
+            rectify(t)
+            if t < PACK - 1:
+                mutate(t, every)
+                epitope(t, every)
 
-        sc = {}
-        for h in range(2):
-            hid = paratope(h)
-            sc[h] = bank(4 + h, [P, N])
+        hid2_codes, hid2_scales = tile("hid2_codes", [P, N], U32), tile("hid2_scales", [P, N], U8)
+        sc = [bank(h, [P, N]) for h in range(2)]
+
+        def score(h, cols):
             nc.tensor.matmul_mx(
-                out=sc[h][:], lhsT=hid[0][:].bitcast(FP8X4), lhsT_scale=hid[1][:],
-                rhs=hid2[0][:].bitcast(FP8X4), rhs_scale=hid2[1][:], start=True, stop=True,
+                out=sc[h][:, cols], lhsT=hid[h][0][:].bitcast(FP8X4), lhsT_scale=hid[h][1][:],
+                rhs=hid2_codes[:, cols].bitcast(FP8X4), rhs_scale=hid2_scales[:, cols], start=True, stop=True,
             )
+
+        for c in range(2):
+            mutate(PACK - 1, slice(256 * c, 256 * (c + 1)))
+            epitope(PACK - 1, slice(256 * c, 256 * (c + 1)))
+        invert(1, "rect3")
+        for c in range(2):
+            cols = slice(256 * c, 256 * (c + 1))
+            quantise("hid2_%d" % c, hid2_rows[:, :, cols], hid2_codes[:, cols], hid2_scales[:, cols])
+            score(0, cols)
+        hid[1] = paratope(1)
+        score(1, every)
         for h in range(2):
             bind = tile("bind%d" % h, [P, N], F32)
             nc.scalar.activation(bind[:], sc[h][:], ACT.Sigmoid, scale=2.0)

@@ -46,19 +46,21 @@ def tile_picked_yglycan_dif_p_kernel(
         ident = tile("ident", [P, P], F32)
         rect = [tile("rect%d" % t, [P, N + SPARE], F32) for t in range(PACK)]
 
-        warm = tile("warm", [P, 1], F32)
-        nc.gpsimd.memset(warm[:], 1.0)
-        warmed = tile("warmed", [P, 1], F32)
-        nc.scalar.activation(warmed[:], warm[:], ACT.Abs_reciprocal_sqrt)
+        es_i32, xs_i32 = es_tab[:].bitcast(I32), xs_tab[:].bitcast(I32)
+        warm, warmed = tile("warm", [P, 1], F32), tile("warmed", [P, 1], F32)
+        nc.gpsimd.memset(ws_raw[1][:], 0)
+        nc.vector.memset(xs_i32, 0)
+        nc.vector.memset(es_i32, 0)
+        nc.vector.memset(warm[:], 1.0)
+        nc.vector.memset(ws_raw[3][:], 0)
+        nc.vector.memset(ws_raw[2][:], 0)
 
         def scale_rows(queue, plane, scales, q):
-            rows = scales[0, 4 * q : 4 * q + 4, :].bitcast(I32)
-            queue.dma_start(out=plane[32 * q : 32 * (q + 1), :], in_=rows.unsqueeze(0).to_broadcast([8, 4, rows.shape[1]]))
+            queue.dma_start(out=plane[32 * q : 32 * q + 4, :], in_=scales[0, 4 * q : 4 * q + 4, :].bitcast(I32))
 
         def table_words(words):
             return words[0].rearrange("p n t -> p (n t)").bitcast(I32)
 
-        es_i32, xs_i32 = es_tab[:].bitcast(I32), xs_tab[:].bitcast(I32)
         def unit_load(queue, name, vec):
             block = tile(name, [P, 32], F32)
             queue.dma_start(out=block[:], in_=vec.rearrange("(b c) o -> b (c o)", c=32).unsqueeze(1).to_broadcast([16, 8, 32]))
@@ -71,15 +73,16 @@ def tile_picked_yglycan_dif_p_kernel(
         for t in range(PACK):
             nc.gpsimd.memset(rect[t][:, N:], 0.0)
         nc.sync.dma_start(lists["offs"][:], offs)
-        for q in range(4):
-            scale_rows(nc.sync, xs_i32, x_scales, q)
         nc.sync.dma_start(out=w_raw[1][:], in_=w1_words[0].bitcast(I32))
-        nc.sync.dma_start(lists["agn"][:], agn)
         nc.sync.dma_start(out=x_tab[:], in_=table_words(x_words))
+        for q in range(4):
+            scale_rows(nc.scalar, xs_i32, x_scales, q)
+        for q in range(4):
+            scale_rows(nc.scalar, es_i32, e_scales, q)
+        nc.scalar.activation(warmed[:], warm[:], ACT.Abs_reciprocal_sqrt)
         for q in range(2):
             scale_rows(nc.sync, ws_raw[1], w1_scales, q)
-        for q in range(4):
-            scale_rows(nc.sync, es_i32, e_scales, q)
+        nc.sync.dma_start(lists["agn"][:], agn)
         nc.sync.dma_start(out=e_tab[:], in_=table_words(e_words))
         nc.sync.dma_start(out=w_raw[3][:], in_=w3_words[0].bitcast(I32))
         for q in range(4):

@@ -48,9 +48,9 @@ def tile_picked_yglycan_dif_p_kernel(
 
         es_i32, xs_i32 = es_tab[:].bitcast(I32), xs_tab[:].bitcast(I32)
         warm, warmed = tile("warm", [P, 1], F32), tile("warmed", [P, 1], F32)
-        nc.gpsimd.memset(ws_raw[1][:], 0)
         nc.vector.memset(xs_i32, 0)
         nc.vector.memset(es_i32, 0)
+        nc.vector.memset(ws_raw[1][:], 0)
         nc.vector.memset(warm[:], 1.0)
         nc.vector.memset(ws_raw[3][:], 0)
         nc.vector.memset(ws_raw[2][:], 0)
@@ -66,8 +66,7 @@ def tile_picked_yglycan_dif_p_kernel(
             queue.dma_start(out=block[:], in_=vec.rearrange("(b c) o -> b (c o)", c=32).unsqueeze(1).to_broadcast([16, 8, 32]))
             return block
 
-        for q in range(2, 4):
-            scale_rows(nc.gpsimd, ws_raw[1], w1_scales, q)
+        unit2_block = unit_load(nc.gpsimd, "unit2_block", unit2)
         unit_block = unit_load(nc.gpsimd, "unit_block", unit)
         make_identity(nc, ident[:])
         for t in range(PACK):
@@ -80,31 +79,35 @@ def tile_picked_yglycan_dif_p_kernel(
         for q in range(4):
             scale_rows(nc.scalar, es_i32, e_scales, q)
         nc.scalar.activation(warmed[:], warm[:], ACT.Abs_reciprocal_sqrt)
-        for q in range(2):
+        for q in range(4):
             scale_rows(nc.sync, ws_raw[1], w1_scales, q)
         nc.sync.dma_start(lists["agn"][:], agn)
         nc.sync.dma_start(out=e_tab[:], in_=table_words(e_words))
         nc.sync.dma_start(out=w_raw[3][:], in_=w3_words[0].bitcast(I32))
         for q in range(4):
             scale_rows(nc.sync, ws_raw[3], w3_scales, q)
-        unit2_block = unit_load(nc.sync, "unit2_block", unit2)
         nc.sync.dma_start(lists["mut"][:], mut)
-        imm_tab = tile("imm_tab", [P, TABLE], F32)
-        nc.sync.dma_start(out=imm_tab[:], in_=imm)
         nc.sync.dma_start(out=w_raw[2][:], in_=w2_words[0].bitcast(I32))
         for q in range(4):
             scale_rows(nc.sync, ws_raw[2], w2_scales, q)
         nc.sync.dma_start(lists["esc"][:], esc)
+        imm_tab = tile("imm_tab", [P, TABLE], F32)
+        nc.sync.dma_start(out=imm_tab[:], in_=imm)
 
-        own = tile("own", [P, 8], F32)
+        def fold(name, values, axis_len):
+            while axis_len > 1:
+                axis_len //= 2
+                halved = tile("%s_%d" % (name, axis_len), [P, values.shape[1], axis_len], F32)
+                nc.gpsimd.tensor_tensor(halved[:], values[:, :, :axis_len], values[:, :, axis_len:], ALU.add)
+                values = halved[:]
+            return values[:, :, 0]
 
-        def own_factors(name, block, slot=None):
-            masked, factors = tile(name + "_masked", [P, PACK, 8], F32, slot), tile(name, [P, PACK], F32)
-            nc.vector.tensor_tensor(
-                masked[:], block[:].rearrange("p (t r) -> p t r", r=8), own[:].unsqueeze(1).to_broadcast([P, PACK, 8]), ALU.mult
+        def own_factors(name, block, own):
+            masked = tile(name + "_masked", [P, PACK, 8], F32)
+            nc.gpsimd.tensor_tensor(
+                masked[:], block[:].rearrange("p (t r) -> p t r", r=8), own.unsqueeze(1).to_broadcast([P, PACK, 8]), ALU.mult
             )
-            nc.vector.tensor_reduce(factors[:], masked[:], mybir.AxisListType.X, ALU.add)
-            return factors
+            return fold(name, masked[:], 8)
 
         def deal(dealt, raw, run):
             nc.vector.tensor_copy(
@@ -135,6 +138,21 @@ def tile_picked_yglycan_dif_p_kernel(
                 stop=True,
             )
 
+        own = fold("own", ident[:].rearrange("p (b r) -> p r b", r=8), 16)
+        u2 = own_factors("u2", unit2_block, own)
+        twice = tile("twice", [P, PACK], F32)
+        sgn = tile("sgn", [P, PACK], F32)
+        mag2 = tile("mag2", [P, PACK], F32)
+        mag2_cut = tile("mag2_cut", [P, PACK], F32)
+        unit_sgn = tile("unit_sgn", [P, PACK], F32)
+        nc.scalar.activation(mag2_cut[:], u2, ACT.Abs, scale=0.8)
+        nc.scalar.activation(mag2[:], u2, ACT.Abs)
+        nc.gpsimd.tensor_scalar(twice[:], u2, 0.0, 2.0, ALU.is_ge, ALU.mult)
+        nc.gpsimd.tensor_scalar(sgn[:], twice[:], -1.0, None, ALU.add)
+
+        u1 = own_factors("u1", unit_block, own)
+        nc.gpsimd.tensor_tensor(unit_sgn[:], u1, sgn[:], ALU.mult)
+
         x_scale_pick = pick("x_scale_pick", xs_tab[:], lists["offs"], U8)
         w1_tile = tile("w1", [P, 3 * N], U8)
         w1_dealt = deal_words(1, w1_tile)
@@ -146,31 +164,30 @@ def tile_picked_yglycan_dif_p_kernel(
                 project(y[h][t // 2][:, t % 2, :], w1, t, x_pick, slice(256 * h, 256 * (h + 1)))
         e_scale_pick = pick("e_scale_pick", es_tab[:], lists["agn"], U8)
 
-        first, size, total, peak, recip = {}, {}, {}, {}, {}
+        first, total, negmax, recip = {}, {}, {}, {}
 
         def members(h, j):
             return y[h][j][:].rearrange("p t (v d) -> p d t v", d=2)
 
         def take(h):
             first[h] = tile("first%d" % h, [P, PACK, P], F32)
-            size[h] = tile("size%d" % h, [P, 2, PACK, P], F32)
             for j in range(2):
-                rows = slice(2 * j, 2 * j + 2)
-                nc.scalar.copy(first[h][:, rows, :], members(h, j)[:, 0])
-                nc.scalar.activation(size[h][:, :, rows, :], members(h, j), ACT.Abs)
+                nc.scalar.copy(first[h][:, 2 * j : 2 * j + 2, :], members(h, j)[:, 0])
 
-        def pairs(h, total_slot, peak_slot):
+        def pairs(h, total_slot, larger_slot):
             total[h] = tile("total%d" % h, [P, PACK, P], F32, total_slot)
-            peak[h] = tile("peak%d" % h, [P, PACK, P], F32, peak_slot)
-            nc.vector.tensor_tensor(peak[h][:], size[h][:, 0], size[h][:, 1], ALU.max)
+            larger = tile("larger%d" % h, [P, PACK, P], F32, larger_slot)
+            negmax[h] = tile("negmax%d" % h, [P, PACK, P], F32)
             for j in range(2):
                 rows = slice(2 * j, 2 * j + 2)
                 nc.vector.tensor_tensor(total[h][:, rows, :], members(h, j)[:, 1], first[h][:, rows, :], ALU.add)
+                nc.vector.tensor_tensor(larger[:, rows, :], members(h, j)[:, 1], first[h][:, rows, :], ALU.max)
+            nc.vector.scalar_tensor_tensor(negmax[h][:], total[h][:], 0.0, larger[:], ALU.min, ALU.subtract)
 
-        def invert(h, slot):
-            root = tile("root%d" % h, [P, PACK, P], F32, slot)
+        def invert(h):
+            root = tile("root%d" % h, [P, PACK, P], F32)
             recip[h] = tile("recip%d" % h, [P, PACK, P], F32)
-            nc.scalar.activation(root[:], peak[h][:], ACT.Abs_reciprocal_sqrt, bias=0.5)
+            nc.scalar.activation(root[:], negmax[h][:], ACT.Abs_reciprocal_sqrt, bias=0.5, scale=-1.0)
             nc.scalar.activation(recip[h][:], root[:], ACT.Square)
 
         def quantise(name, rows, codes, scales):
@@ -182,8 +199,8 @@ def tile_picked_yglycan_dif_p_kernel(
             )
             nc.vector.quantize_mx(out=codes.bitcast(FP8X4), scales=scales, in_=woven[:].rearrange("p w t -> p (w t)"))
 
-        def paratope(h):
-            rows = tile("hid_rows%d" % h, [P, PACK, P], BF16)
+        def paratope(h, slot):
+            rows = tile("hid_rows%d" % h, [P, PACK, P], BF16, slot)
             for t in range(PACK):
                 nc.vector.scalar_tensor_tensor(rows[:, t, :], total[h][:, t, :], unit_sgn[:, t : t + 1], recip[h][:, t, :], ALU.mult, ALU.mult)
             codes, scales = tile("hid_codes%d" % h, [P, P], U32), tile("hid_scales%d" % h, [P, P], U8)
@@ -196,28 +213,13 @@ def tile_picked_yglycan_dif_p_kernel(
         w3_tile = tile("w3", [P, 3 * N], U8)
         w3 = (deal_words(3, w3_tile), deal_scales(3, w3_tile))
 
-        nc.vector.tensor_reduce(own[:], ident[:].rearrange("p (b r) -> p r b", r=8), mybir.AxisListType.X, ALU.add)
-        u2 = own_factors("u2", unit2_block)
-        twice = tile("twice", [P, PACK], F32)
-        sgn = tile("sgn", [P, PACK], F32)
-        mag2 = tile("mag2", [P, PACK], F32)
-        mag2_cut = tile("mag2_cut", [P, PACK], F32)
-        unit_sgn = tile("unit_sgn", [P, PACK], F32)
-        nc.scalar.activation(mag2_cut[:], u2[:], ACT.Abs, scale=0.8)
-        nc.scalar.activation(mag2[:], u2[:], ACT.Abs)
-        nc.gpsimd.tensor_scalar(twice[:], u2[:], 0.0, 2.0, ALU.is_ge, ALU.mult)
-        nc.gpsimd.tensor_scalar(sgn[:], twice[:], -1.0, None, ALU.add)
-
         every = slice(0, N)
         yw = [bank(t, [P, N]) for t in range(PACK)]
         for t in range(PACK):
             project(yw[t][:], w3, t, e_pick, every)
-        pairs(0, "w3s_raw", "u2_masked")
-        u1 = own_factors("u1", unit_block, "w3_raw")
-        nc.gpsimd.tensor_tensor(unit_sgn[:], u1[:], sgn[:], ALU.mult)
-        pairs(1, "unit2_block", "size0")
-        imm_pick = tile("imm_pick", [P, N], F32, slot="first0")
-        nc.vector.tensor_copy(imm_pick[:], imm_tab[:].indirect(lists["agn"][:]))
+        pairs(0, None, None)
+        invert(0)
+        pairs(1, "w3s_raw", "w3_raw")
         w2_tile = tile("w2", [P, 3 * N], U8, slot="first1")
         w2 = (deal_words(2, w2_tile), deal_scales(2, w2_tile))
         ye = [bank(4 + t, [P, N]) for t in range(PACK)]
@@ -239,16 +241,19 @@ def tile_picked_yglycan_dif_p_kernel(
                 hid2_rows[:, t, cols], ye[t][:, cols], mag2[:, t : t + 1], mutated[t][:, cols], ALU.mult, ALU.subtract
             )
 
+        hid = {0: paratope(0, None)}
         rectify(0)
+        rectify(1)
         mutate(0, every)
-        invert(0, "rect0")
-        hid = {0: paratope(0)}
         epitope(0, every)
-        for t in range(1, PACK):
-            rectify(t)
-            if t < PACK - 1:
-                mutate(t, every)
-                epitope(t, every)
+        rectify(2)
+        mutate(1, every)
+        epitope(1, every)
+        invert(1)
+        rectify(3)
+        mutate(2, every)
+        hid[1] = paratope(1, "mutated0")
+        epitope(2, every)
 
         hid2_codes, hid2_scales = tile("hid2_codes", [P, N], U32), tile("hid2_scales", [P, N], U8)
         sc = [bank(h, [P, N]) for h in range(2)]
@@ -262,12 +267,12 @@ def tile_picked_yglycan_dif_p_kernel(
         for c in range(2):
             mutate(PACK - 1, slice(256 * c, 256 * (c + 1)))
             epitope(PACK - 1, slice(256 * c, 256 * (c + 1)))
-        invert(1, "rect3")
+        imm_pick = tile("imm_pick", [P, N], F32, slot="rect3")
+        nc.scalar.activation(imm_pick[:], imm_tab[:].indirect(lists["agn"][:]), ACT.Copy)
         for c in range(2):
             cols = slice(256 * c, 256 * (c + 1))
             quantise("hid2_%d" % c, hid2_rows[:, :, cols], hid2_codes[:, cols], hid2_scales[:, cols])
             score(0, cols)
-        hid[1] = paratope(1)
         score(1, every)
         for h in range(2):
             bind = tile("bind%d" % h, [P, N], F32)

@@ -17,7 +17,12 @@ ACT = mybir.ActivationFunctionType
 P = 128
 TABLE = 2048
 N = 512
+HALF = N // 2
 PACK = 4
+RUN = 8
+BLOCK = RUN * PACK
+QUADS = P // BLOCK
+PER_COLUMN = 16
 SPARE = 16
 FLOPS = 939524096
 
@@ -37,58 +42,60 @@ def tile_picked_yglycan_dif_p_kernel(
         def bank(index, shape):
             return ps.tile(shape, F32, name="bank%d" % index, tag="bank%d" % index)
 
-        lists = {name: tile(name + "_list", [P, N // 16], U16) for name in ("agn", "offs", "mut", "esc")}
+        lists = {name: tile(name + "_list", [P, N // PER_COLUMN], U16) for name in ("agn", "offs", "mut", "esc")}
         e_tab, x_tab = tile("e_tab", [P, TABLE], I32), tile("x_tab", [P, TABLE], I32)
         es_tab, xs_tab = tile("es_tab", [P, TABLE], U8), tile("xs_tab", [P, TABLE], U8)
-        w_raw = {w: tile("w%d_raw" % w, [P, 256], I32) for w in (1, 2, 3)}
-        ws_raw = {w: tile("w%ds_raw" % w, [P, 128], I32) for w in (1, 2, 3)}
-
+        w_raw = {w: tile("w%d_raw" % w, [P, 2 * N // 4], I32) for w in (1, 2, 3)}
+        ws_raw = {w: tile("w%ds_raw" % w, [P, N // 4], I32) for w in (1, 2, 3)}
         ident = tile("ident", [P, P], F32)
         rect = [tile("rect%d" % t, [P, N + SPARE], F32) for t in range(PACK)]
 
         es_i32, xs_i32 = es_tab[:].bitcast(I32), xs_tab[:].bitcast(I32)
         warm, warmed = tile("warm", [P, 1], F32), tile("warmed", [P, 1], F32)
+        nc.gpsimd.memset(ws_raw[1][:], 0)
         nc.vector.memset(xs_i32, 0)
-        nc.vector.memset(es_i32, 0)
-        nc.vector.memset(ws_raw[1][:], 0)
         nc.vector.memset(warm[:], 1.0)
+        nc.vector.memset(es_i32, 0)
         nc.vector.memset(ws_raw[3][:], 0)
         nc.vector.memset(ws_raw[2][:], 0)
 
         def scale_rows(queue, plane, scales, q):
-            queue.dma_start(out=plane[32 * q : 32 * q + 4, :], in_=scales[0, 4 * q : 4 * q + 4, :].bitcast(I32))
+            queue.dma_start(out=plane[BLOCK * q : BLOCK * q + 4, :], in_=scales[0, 4 * q : 4 * q + 4, :].bitcast(I32))
 
         def table_words(words):
             return words[0].rearrange("p n t -> p (n t)").bitcast(I32)
 
-        def unit_load(queue, name, vec):
-            block = tile(name, [P, 32], F32)
-            queue.dma_start(out=block[:], in_=vec.rearrange("(b c) o -> b (c o)", c=32).unsqueeze(1).to_broadcast([16, 8, 32]))
+        def unit_load(name, vec):
+            block = tile(name, [P, BLOCK], F32)
+            rows = vec.rearrange("(b c) o -> b (c o)", c=BLOCK)
+            nc.gpsimd.dma_start(out=block[:], in_=rows.unsqueeze(1).to_broadcast([P // RUN, RUN, BLOCK]))
             return block
 
-        unit2_block = unit_load(nc.gpsimd, "unit2_block", unit2)
-        unit_block = unit_load(nc.gpsimd, "unit_block", unit)
+        for q in range(QUADS // 2, QUADS):
+            scale_rows(nc.gpsimd, ws_raw[1], w1_scales, q)
+        unit2_block = unit_load("unit2_block", unit2)
+        unit_block = unit_load("unit_block", unit)
         make_identity(nc, ident[:])
         for t in range(PACK):
             nc.gpsimd.memset(rect[t][:, N:], 0.0)
         nc.sync.dma_start(lists["offs"][:], offs)
         nc.sync.dma_start(out=w_raw[1][:], in_=w1_words[0].bitcast(I32))
         nc.sync.dma_start(out=x_tab[:], in_=table_words(x_words))
-        for q in range(4):
+        for q in range(QUADS):
             scale_rows(nc.scalar, xs_i32, x_scales, q)
-        for q in range(4):
-            scale_rows(nc.scalar, es_i32, e_scales, q)
+        for q in range(QUADS // 2):
+            scale_rows(nc.scalar, ws_raw[1], w1_scales, q)
         nc.scalar.activation(warmed[:], warm[:], ACT.Abs_reciprocal_sqrt)
-        for q in range(4):
-            scale_rows(nc.sync, ws_raw[1], w1_scales, q)
-        nc.sync.dma_start(lists["agn"][:], agn)
         nc.sync.dma_start(out=e_tab[:], in_=table_words(e_words))
+        nc.sync.dma_start(lists["agn"][:], agn)
+        for q in range(QUADS):
+            scale_rows(nc.sync, es_i32, e_scales, q)
         nc.sync.dma_start(out=w_raw[3][:], in_=w3_words[0].bitcast(I32))
-        for q in range(4):
+        for q in range(QUADS):
             scale_rows(nc.sync, ws_raw[3], w3_scales, q)
         nc.sync.dma_start(lists["mut"][:], mut)
         nc.sync.dma_start(out=w_raw[2][:], in_=w2_words[0].bitcast(I32))
-        for q in range(4):
+        for q in range(QUADS):
             scale_rows(nc.sync, ws_raw[2], w2_scales, q)
         nc.sync.dma_start(lists["esc"][:], esc)
         imm_tab = tile("imm_tab", [P, TABLE], F32)
@@ -103,11 +110,11 @@ def tile_picked_yglycan_dif_p_kernel(
             return values[:, :, 0]
 
         def own_factors(name, block, own):
-            masked = tile(name + "_masked", [P, PACK, 8], F32)
+            masked = tile(name + "_masked", [P, PACK, RUN], F32)
             nc.gpsimd.tensor_tensor(
-                masked[:], block[:].rearrange("p (t r) -> p t r", r=8), own.unsqueeze(1).to_broadcast([P, PACK, 8]), ALU.mult
+                masked[:], block[:].rearrange("p (t r) -> p t r", r=RUN), own.unsqueeze(1).to_broadcast([P, PACK, RUN]), ALU.mult
             )
-            return fold(name, masked[:], 8)
+            return fold(name, masked[:], RUN)
 
         def deal(dealt, raw, run):
             nc.vector.tensor_copy(
@@ -117,13 +124,13 @@ def tile_picked_yglycan_dif_p_kernel(
             return dealt
 
         def deal_words(w, dealt):
-            return deal(dealt[:, : 2 * N], w_raw[w], 4)
+            return deal(dealt[:, : 2 * N], w_raw[w], 2 * RUN // 4)
 
         def deal_scales(w, dealt):
-            return deal(dealt[:, 2 * N :], ws_raw[w], 2)
+            return deal(dealt[:, 2 * N :], ws_raw[w], RUN // 4)
 
-        def pick(name, window, offsets, dtype):
-            picked = tile(name, [P, N], dtype)
+        def pick(name, window, offsets, dtype, slot=None):
+            picked = tile(name, [P, N], dtype, slot)
             nc.vector.tensor_copy(picked[:], window.indirect(offsets[:]))
             return picked
 
@@ -138,7 +145,7 @@ def tile_picked_yglycan_dif_p_kernel(
                 stop=True,
             )
 
-        own = fold("own", ident[:].rearrange("p (b r) -> p r b", r=8), 16)
+        own = fold("own", ident[:].rearrange("p (b r) -> p r b", r=RUN), P // RUN)
         u2 = own_factors("u2", unit2_block, own)
         twice = tile("twice", [P, PACK], F32)
         sgn = tile("sgn", [P, PACK], F32)
@@ -149,7 +156,6 @@ def tile_picked_yglycan_dif_p_kernel(
         nc.scalar.activation(mag2[:], u2, ACT.Abs)
         nc.gpsimd.tensor_scalar(twice[:], u2, 0.0, 2.0, ALU.is_ge, ALU.mult)
         nc.gpsimd.tensor_scalar(sgn[:], twice[:], -1.0, None, ALU.add)
-
         u1 = own_factors("u1", unit_block, own)
         nc.gpsimd.tensor_tensor(unit_sgn[:], u1, sgn[:], ALU.mult)
 
@@ -158,11 +164,11 @@ def tile_picked_yglycan_dif_p_kernel(
         w1_dealt = deal_words(1, w1_tile)
         x_pick = (pick("x_pick", x_tab[:].bitcast(U32), lists["offs"], U32), x_scale_pick)
         w1 = (w1_dealt, deal_scales(1, w1_tile))
-        y = [[bank(4 + 2 * h + j, [P, 2, N // 2]) for j in range(2)] for h in range(2)]
+        y = [[bank(PACK + 2 * h + j, [P, 2, HALF]) for j in range(2)] for h in range(2)]
         for h in range(2):
             for t in range(PACK):
-                project(y[h][t // 2][:, t % 2, :], w1, t, x_pick, slice(256 * h, 256 * (h + 1)))
-        e_scale_pick = pick("e_scale_pick", es_tab[:], lists["agn"], U8)
+                project(y[h][t // 2][:, t % 2, :], w1, t, x_pick, slice(HALF * h, HALF * (h + 1)))
+        e_scale_pick = pick("e_scale_pick", es_tab[:], lists["agn"], U8, "w1s_raw")
 
         first, total, negmax, recip = {}, {}, {}, {}
 
@@ -202,7 +208,9 @@ def tile_picked_yglycan_dif_p_kernel(
         def paratope(h, slot):
             rows = tile("hid_rows%d" % h, [P, PACK, P], BF16, slot)
             for t in range(PACK):
-                nc.vector.scalar_tensor_tensor(rows[:, t, :], total[h][:, t, :], unit_sgn[:, t : t + 1], recip[h][:, t, :], ALU.mult, ALU.mult)
+                nc.vector.scalar_tensor_tensor(
+                    rows[:, t, :], total[h][:, t, :], unit_sgn[:, t : t + 1], recip[h][:, t, :], ALU.mult, ALU.mult
+                )
             codes, scales = tile("hid_codes%d" % h, [P, P], U32), tile("hid_scales%d" % h, [P, P], U8)
             quantise("hid%d" % h, rows[:], codes[:], scales[:])
             return codes, scales
@@ -217,34 +225,36 @@ def tile_picked_yglycan_dif_p_kernel(
         yw = [bank(t, [P, N]) for t in range(PACK)]
         for t in range(PACK):
             project(yw[t][:], w3, t, e_pick, every)
-        pairs(0, None, None)
-        invert(0)
-        pairs(1, "w3s_raw", "w3_raw")
+        pairs(0, "w3s_raw", "w3_raw")
+        pairs(1, "first0", "w3_raw")
         w2_tile = tile("w2", [P, 3 * N], U8, slot="first1")
         w2 = (deal_words(2, w2_tile), deal_scales(2, w2_tile))
-        ye = [bank(4 + t, [P, N]) for t in range(PACK)]
+        ye = [bank(PACK + t, [P, N]) for t in range(PACK)]
         for t in range(PACK):
             project(ye[t][:], w2, t, e_pick, every)
 
         mutated = [tile("mutated%d" % t, [P, N], F32) for t in range(PACK)]
         hid2_rows = tile("hid2_rows", [P, PACK, N], BF16)
 
+        def entries(name, cols):
+            return lists[name][:, cols.start // PER_COLUMN : cols.stop // PER_COLUMN]
+
         def rectify(t):
             nc.scalar.activation(rect[t][:, :N], yw[t][:], ACT.Relu, scale=mag2_cut[:, t : t + 1])
 
         def mutate(t, cols):
-            offsets = lists["mut"][:, cols.start // 16 : cols.stop // 16]
-            nc.scalar.activation(mutated[t][:, cols], rect[t][:].indirect(offsets), ACT.Copy)
+            nc.scalar.activation(mutated[t][:, cols], rect[t][:].indirect(entries("mut", cols)), ACT.Copy)
 
         def epitope(t, cols):
             nc.vector.scalar_tensor_tensor(
                 hid2_rows[:, t, cols], ye[t][:, cols], mag2[:, t : t + 1], mutated[t][:, cols], ALU.mult, ALU.subtract
             )
 
-        hid = {0: paratope(0, None)}
         rectify(0)
         rectify(1)
         mutate(0, every)
+        invert(0)
+        hid = {0: paratope(0, None)}
         epitope(0, every)
         rectify(2)
         mutate(1, every)
@@ -264,27 +274,27 @@ def tile_picked_yglycan_dif_p_kernel(
                 rhs=hid2_codes[:, cols].bitcast(FP8X4), rhs_scale=hid2_scales[:, cols], start=True, stop=True,
             )
 
-        for c in range(2):
-            mutate(PACK - 1, slice(256 * c, 256 * (c + 1)))
-            epitope(PACK - 1, slice(256 * c, 256 * (c + 1)))
+        halves = [slice(HALF * c, HALF * (c + 1)) for c in range(2)]
+        for cols in halves:
+            mutate(PACK - 1, cols)
+            epitope(PACK - 1, cols)
         imm_pick = tile("imm_pick", [P, N], F32, slot="rect3")
         nc.scalar.activation(imm_pick[:], imm_tab[:].indirect(lists["agn"][:]), ACT.Copy)
-        for c in range(2):
-            cols = slice(256 * c, 256 * (c + 1))
+        for c, cols in enumerate(halves):
             quantise("hid2_%d" % c, hid2_rows[:, :, cols], hid2_codes[:, cols], hid2_scales[:, cols])
             score(0, cols)
         score(1, every)
+
         for h in range(2):
             bind = tile("bind%d" % h, [P, N], F32)
             nc.scalar.activation(bind[:], sc[h][:], ACT.Sigmoid, scale=2.0)
-            for c in range(2):
-                cols = slice(256 * c, 256 * (c + 1))
+            for c, cols in enumerate(halves):
                 name = "%d_%d" % (h, c)
-                escaped = tile("escaped" + name, [P, 256], F32)
-                drop = tile("drop" + name, [P, 256], F32)
-                weighed = tile("weighed" + name, [P, 256], F32)
-                result = tile("result" + name, [P, 256], F32)
-                nc.scalar.activation(escaped[:], bind[:].indirect(lists["esc"][:, 16 * c : 16 * (c + 1)]), ACT.Copy)
+                escaped = tile("escaped" + name, [P, HALF], F32)
+                drop = tile("drop" + name, [P, HALF], F32)
+                weighed = tile("weighed" + name, [P, HALF], F32)
+                result = tile("result" + name, [P, HALF], F32)
+                nc.scalar.activation(escaped[:], bind[:].indirect(entries("esc", cols)), ACT.Copy)
                 nc.vector.tensor_tensor(drop[:], bind[:, cols], escaped[:], ALU.subtract)
                 nc.vector.tensor_tensor(weighed[:], drop[:], imm_pick[:, cols], ALU.mult)
                 nc.vector.scalar_tensor_tensor(result[:], sc[h][:, cols], 0.2, weighed[:], ALU.mult, ALU.add)

from contextlib import ExitStack

import concourse.mybir as mybir
from concourse.masks import make_identity

F32 = mybir.dt.float32
BF16 = mybir.dt.bfloat16
I32 = mybir.dt.int32
U32 = mybir.dt.uint32
U16 = mybir.dt.uint16
U8 = mybir.dt.uint8
FP8X4 = mybir.dt.float8_e4m3fn_x4
FP4X4 = mybir.dt.float4_e2m1fn_x4
ALU = mybir.AluOpType
ACT = mybir.ActivationFunctionType

P = 128
TABLE = 2048
N = 512
HALF = N // 2
PACK = 4
RUN = 8
BLOCK = RUN * PACK
QUADS = P // BLOCK
PER_COLUMN = 16
SPARE = 16
FLOPS = 939524096


def tile_picked_yglycan_dif_p_kernel(
    tc, x_words, x_scales, w1_words, w1_scales, e_words, e_scales, w2_words, w2_scales,
    w3_words, w3_scales, unit, unit2, imm, offs, agn, mut, esc, out,
):
    nc = tc.nc
    with ExitStack() as ctx:
        sb = ctx.enter_context(tc.tile_pool(name="sb", bufs=1))
        ps = ctx.enter_context(tc.psum_pool(name="ps", bufs=1))

        def tile(name, shape, dtype, slot=None):
            return sb.tile(shape, dtype, name=name, tag=slot or name, align_bytes=64)

        def bank(index, shape):
            return ps.tile(shape, F32, name="bank%d" % index, tag="bank%d" % index)

        lists = {name: tile(name + "_list", [P, N // PER_COLUMN], U16) for name in ("agn", "offs", "mut", "esc")}
        e_tab, x_tab = tile("e_tab", [P, TABLE], I32), tile("x_tab", [P, TABLE], I32)
        es_tab, xs_tab = tile("es_tab", [P, TABLE], U8), tile("xs_tab", [P, TABLE], U8)
        w_raw = {w: tile("w%d_raw" % w, [P, 2 * N // 4], I32) for w in (1, 2, 3)}
        ws_raw = {w: tile("w%ds_raw" % w, [P, N // 4], I32) for w in (1, 2, 3)}
        ident = tile("ident", [P, P], F32)
        rect = [tile("rect%d" % t, [P, N + SPARE], F32) for t in range(PACK)]

        es_i32, xs_i32 = es_tab[:].bitcast(I32), xs_tab[:].bitcast(I32)
        warm, warmed = tile("warm", [P, 1], F32), tile("warmed", [P, 1], F32)
        nc.gpsimd.memset(ws_raw[1][:], 0)
        nc.vector.memset(xs_i32, 0)
        nc.vector.memset(warm[:], 1.0)
        nc.vector.memset(es_i32, 0)
        nc.vector.memset(ws_raw[3][:], 0)
        nc.vector.memset(ws_raw[2][:], 0)

        def scale_rows(queue, plane, scales, q):
            queue.dma_start(out=plane[BLOCK * q : BLOCK * q + 4, :], in_=scales[0, 4 * q : 4 * q + 4, :].bitcast(I32))

        def table_words(words):
            return words[0].rearrange("p n t -> p (n t)").bitcast(I32)

        def unit_load(name, vec):
            block = tile(name, [P, BLOCK], F32)
            rows = vec.rearrange("(b c) o -> b (c o)", c=BLOCK)
            nc.gpsimd.dma_start(out=block[:], in_=rows.unsqueeze(1).to_broadcast([P // RUN, RUN, BLOCK]))
            return block

        for q in range(QUADS // 2, QUADS):
            scale_rows(nc.gpsimd, ws_raw[1], w1_scales, q)
        unit2_block = unit_load("unit2_block", unit2)
        unit_block = unit_load("unit_block", unit)
        make_identity(nc, ident[:])
        for t in range(PACK):
            nc.gpsimd.memset(rect[t][:, N:], 0.0)
        nc.sync.dma_start(lists["offs"][:], offs)
        nc.sync.dma_start(out=w_raw[1][:], in_=w1_words[0].bitcast(I32))
        nc.sync.dma_start(out=x_tab[:], in_=table_words(x_words))
        for q in range(QUADS):
            scale_rows(nc.scalar, xs_i32, x_scales, q)
        for q in range(QUADS // 2):
            scale_rows(nc.scalar, ws_raw[1], w1_scales, q)
        nc.scalar.activation(warmed[:], warm[:], ACT.Abs_reciprocal_sqrt)
        nc.sync.dma_start(out=e_tab[:], in_=table_words(e_words))
        nc.sync.dma_start(lists["agn"][:], agn)
        for q in range(QUADS):
            scale_rows(nc.sync, es_i32, e_scales, q)
        nc.sync.dma_start(out=w_raw[3][:], in_=w3_words[0].bitcast(I32))
        for q in range(QUADS):
            scale_rows(nc.sync, ws_raw[3], w3_scales, q)
        nc.sync.dma_start(lists["mut"][:], mut)
        nc.sync.dma_start(out=w_raw[2][:], in_=w2_words[0].bitcast(I32))
        for q in range(QUADS):
            scale_rows(nc.sync, ws_raw[2], w2_scales, q)
        nc.sync.dma_start(lists["esc"][:], esc)
        imm_tab = tile("imm_tab", [P, TABLE], F32)
        nc.sync.dma_start(out=imm_tab[:], in_=imm)

        def fold(name, values, axis_len):
            while axis_len > 1:
                axis_len //= 2
                halved = tile("%s_%d" % (name, axis_len), [P, values.shape[1], axis_len], F32)
                nc.gpsimd.tensor_tensor(halved[:], values[:, :, :axis_len], values[:, :, axis_len:], ALU.add)
                values = halved[:]
            return values[:, :, 0]

        def own_factors(name, block, own):
            masked = tile(name + "_masked", [P, PACK, RUN], F32)
            nc.gpsimd.tensor_tensor(
                masked[:], block[:].rearrange("p (t r) -> p t r", r=RUN), own.unsqueeze(1).to_broadcast([P, PACK, RUN]), ALU.mult
            )
            return fold(name, masked[:], RUN)

        def deal(dealt, raw, run):
            nc.vector.tensor_copy(
                out=dealt.bitcast(I32).rearrange("p (t b c) -> p t b c", t=PACK, c=run),
                in_=raw[:].rearrange("p (b t c) -> p t b c", t=PACK, c=run),
            )
            return dealt

        def deal_words(w, dealt):
            return deal(dealt[:, : 2 * N], w_raw[w], 2 * RUN // 4)

        def deal_scales(w, dealt):
            return deal(dealt[:, 2 * N :], ws_raw[w], RUN // 4)

        def pick(name, window, offsets, dtype, slot=None):
            picked = tile(name, [P, N], dtype, slot)
            nc.vector.tensor_copy(picked[:], window.indirect(offsets[:]))
            return picked

        def project(dst, weight, t, picked, cols):
            nc.tensor.matmul_mx(
                out=dst,
                lhsT=weight[0][:, 2 * P * t : 2 * P * (t + 1)].bitcast(FP4X4),
                lhsT_scale=weight[1][:, P * t : P * (t + 1)],
                rhs=picked[0][:, cols].bitcast(FP8X4),
                rhs_scale=picked[1][:, cols],
                start=True,
                stop=True,
            )

        own = fold("own", ident[:].rearrange("p (b r) -> p r b", r=RUN), P // RUN)
        u2 = own_factors("u2", unit2_block, own)
        twice = tile("twice", [P, PACK], F32)
        sgn = tile("sgn", [P, PACK], F32)
        mag2 = tile("mag2", [P, PACK], F32)
        mag2_cut = tile("mag2_cut", [P, PACK], F32)
        unit_sgn = tile("unit_sgn", [P, PACK], F32)
        nc.scalar.activation(mag2_cut[:], u2, ACT.Abs, scale=0.8)
        nc.scalar.activation(mag2[:], u2, ACT.Abs)
        nc.gpsimd.tensor_scalar(twice[:], u2, 0.0, 2.0, ALU.is_ge, ALU.mult)
        nc.gpsimd.tensor_scalar(sgn[:], twice[:], -1.0, None, ALU.add)
        u1 = own_factors("u1", unit_block, own)
        nc.gpsimd.tensor_tensor(unit_sgn[:], u1, sgn[:], ALU.mult)

        x_scale_pick = pick("x_scale_pick", xs_tab[:], lists["offs"], U8)
        w1_tile = tile("w1", [P, 3 * N], U8)
        w1_dealt = deal_words(1, w1_tile)
        x_pick = (pick("x_pick", x_tab[:].bitcast(U32), lists["offs"], U32), x_scale_pick)
        w1 = (w1_dealt, deal_scales(1, w1_tile))
        y = [[bank(PACK + 2 * h + j, [P, 2, HALF]) for j in range(2)] for h in range(2)]
        for h in range(2):
            for t in range(PACK):
                project(y[h][t // 2][:, t % 2, :], w1, t, x_pick, slice(HALF * h, HALF * (h + 1)))
        e_scale_pick = pick("e_scale_pick", es_tab[:], lists["agn"], U8, "w1s_raw")

        first, total, negmax, recip = {}, {}, {}, {}

        def members(h, j):
            return y[h][j][:].rearrange("p t (v d) -> p d t v", d=2)

        def take(h):
            first[h] = tile("first%d" % h, [P, PACK, P], F32)
            for j in range(2):
                nc.scalar.copy(first[h][:, 2 * j : 2 * j + 2, :], members(h, j)[:, 0])

        def pairs(h, total_slot, larger_slot):
            total[h] = tile("total%d" % h, [P, PACK, P], F32, total_slot)
            larger = tile("larger%d" % h, [P, PACK, P], F32, larger_slot)
            negmax[h] = tile("negmax%d" % h, [P, PACK, P], F32)
            for j in range(2):
                rows = slice(2 * j, 2 * j + 2)
                nc.vector.tensor_tensor(total[h][:, rows, :], members(h, j)[:, 1], first[h][:, rows, :], ALU.add)
                nc.vector.tensor_tensor(larger[:, rows, :], members(h, j)[:, 1], first[h][:, rows, :], ALU.max)
            nc.vector.scalar_tensor_tensor(negmax[h][:], total[h][:], 0.0, larger[:], ALU.min, ALU.subtract)

        def invert(h):
            root = tile("root%d" % h, [P, PACK, P], F32)
            recip[h] = tile("recip%d" % h, [P, PACK, P], F32)
            nc.scalar.activation(root[:], negmax[h][:], ACT.Abs_reciprocal_sqrt, bias=0.5, scale=-1.0)
            nc.scalar.activation(recip[h][:], root[:], ACT.Square)

        def quantise(name, rows, codes, scales):
            width = rows.shape[2]
            woven = tile(name + "_woven", [P, width, PACK], BF16)
            nc.vector.tensor_copy(
                out=woven[:].rearrange("p (c i) t -> p c t i", i=4),
                in_=rows.rearrange("p t (c i) -> p c t i", i=4),
            )
            nc.vector.quantize_mx(out=codes.bitcast(FP8X4), scales=scales, in_=woven[:].rearrange("p w t -> p (w t)"))

        def paratope(h, slot):
            rows = tile("hid_rows%d" % h, [P, PACK, P], BF16, slot)
            for t in range(PACK):
                nc.vector.scalar_tensor_tensor(
                    rows[:, t, :], total[h][:, t, :], unit_sgn[:, t : t + 1], recip[h][:, t, :], ALU.mult, ALU.mult
                )
            codes, scales = tile("hid_codes%d" % h, [P, P], U32), tile("hid_scales%d" % h, [P, P], U8)
            quantise("hid%d" % h, rows[:], codes[:], scales[:])
            return codes, scales

        take(0)
        take(1)
        e_pick = (pick("e_pick", e_tab[:].bitcast(U32), lists["agn"], U32), e_scale_pick)
        w3_tile = tile("w3", [P, 3 * N], U8)
        w3 = (deal_words(3, w3_tile), deal_scales(3, w3_tile))

        every = slice(0, N)
        yw = [bank(t, [P, N]) for t in range(PACK)]
        for t in range(PACK):
            project(yw[t][:], w3, t, e_pick, every)
        pairs(0, "w3s_raw", "w3_raw")
        pairs(1, "first0", "w3_raw")
        w2_tile = tile("w2", [P, 3 * N], U8, slot="first1")
        w2 = (deal_words(2, w2_tile), deal_scales(2, w2_tile))
        ye = [bank(PACK + t, [P, N]) for t in range(PACK)]
        for t in range(PACK):
            project(ye[t][:], w2, t, e_pick, every)

        mutated = [tile("mutated%d" % t, [P, N], F32) for t in range(PACK)]
        hid2_rows = tile("hid2_rows", [P, PACK, N], BF16)

        def entries(name, cols):
            return lists[name][:, cols.start // PER_COLUMN : cols.stop // PER_COLUMN]

        def rectify(t):
            nc.scalar.activation(rect[t][:, :N], yw[t][:], ACT.Relu, scale=mag2_cut[:, t : t + 1])

        def mutate(t, cols):
            nc.scalar.activation(mutated[t][:, cols], rect[t][:].indirect(entries("mut", cols)), ACT.Copy)

        def epitope(t, cols):
            nc.vector.scalar_tensor_tensor(
                hid2_rows[:, t, cols], ye[t][:, cols], mag2[:, t : t + 1], mutated[t][:, cols], ALU.mult, ALU.subtract
            )

        rectify(0)
        rectify(1)
        mutate(0, every)
        invert(0)
        hid = {0: paratope(0, None)}
        epitope(0, every)
        rectify(2)
        mutate(1, every)
        epitope(1, every)
        invert(1)
        rectify(3)
        mutate(2, every)
        hid[1] = paratope(1, "mutated0")
        epitope(2, every)

        hid2_codes, hid2_scales = tile("hid2_codes", [P, N], U32), tile("hid2_scales", [P, N], U8)
        sc = [bank(h, [P, N]) for h in range(2)]

        def score(h, cols):
            nc.tensor.matmul_mx(
                out=sc[h][:, cols], lhsT=hid[h][0][:].bitcast(FP8X4), lhsT_scale=hid[h][1][:],
                rhs=hid2_codes[:, cols].bitcast(FP8X4), rhs_scale=hid2_scales[:, cols], start=True, stop=True,
            )

        halves = [slice(HALF * c, HALF * (c + 1)) for c in range(2)]
        for cols in halves:
            mutate(PACK - 1, cols)
            epitope(PACK - 1, cols)
        imm_pick = tile("imm_pick", [P, N], F32, slot="rect3")
        nc.scalar.activation(imm_pick[:], imm_tab[:].indirect(lists["agn"][:]), ACT.Copy)
        for c, cols in enumerate(halves):
            quantise("hid2_%d" % c, hid2_rows[:, :, cols], hid2_codes[:, cols], hid2_scales[:, cols])
            score(0, cols)
        score(1, every)

        for h in range(2):
            bind = tile("bind%d" % h, [P, N], F32)
            nc.scalar.activation(bind[:], sc[h][:], ACT.Sigmoid, scale=2.0)
            for c, cols in enumerate(halves):
                name = "%d_%d" % (h, c)
                escaped = tile("escaped" + name, [P, HALF], F32)
                drop = tile("drop" + name, [P, HALF], F32)
                weighed = tile("weighed" + name, [P, HALF], F32)
                result = tile("result" + name, [P, HALF], F32)
                nc.scalar.activation(escaped[:], bind[:].indirect(entries("esc", cols)), ACT.Copy)
                nc.vector.tensor_tensor(drop[:], bind[:, cols], escaped[:], ALU.subtract)
                nc.vector.tensor_tensor(weighed[:], drop[:], imm_pick[:, cols], ALU.mult)
                nc.vector.scalar_tensor_tensor(result[:], sc[h][:, cols], 0.2, weighed[:], ALU.mult, ALU.add)
                nc.sync.dma_start(out=out[P * h : P * (h + 1), cols], in_=result[:])
